import numpy as np
import ml_dtypes


def mxq(x, axis, fmt="e4m3"):
    dtype, down = {"e4m3": (ml_dtypes.float8_e4m3fn, 7), "e5m2": (ml_dtypes.float8_e5m2, 14)}[fmt]
    v = np.moveaxis(np.asarray(x, np.float32).astype(ml_dtypes.bfloat16).astype(np.float64), axis, -1)
    blocks = v.reshape(v.shape[:-1] + (-1, 32))
    amax = np.abs(blocks).max(-1, keepdims=True)
    byte = np.maximum(np.where(amax > 0, np.frexp(amax)[1] - 1 + 127, 0) - down, 1)
    scale = np.exp2(byte - 127.0)
    codes = (blocks / scale).astype(np.float32).astype(dtype).astype(np.float64)
    return np.moveaxis((codes * scale).reshape(v.shape), -1, axis)


WIDE = False


def mx_kscale(k):
    if not WIDE:
        return np.ones(k)
    levels = np.array([10, -10, 5, -5, 0])
    if k % 512:
        return np.exp2(np.random.permutation(np.resize(levels, k // 32))).repeat(32)
    a = np.empty((k // 512, 16))
    for p in range(k // 512):
        a[p, :8] = np.random.permutation(np.resize(levels, 8))
        for g in range(8):
            far = levels[np.abs(levels - a[p, g]) >= 10]
            a[p, g + 8] = far[np.random.randint(len(far))]
    return np.exp2(a.ravel()).repeat(32)


def f64(x):
    return np.asarray(x).astype(np.float64)


def striped(idx):
    return np.tile(idx.reshape(-1, 16).T, (8, 1)).astype(np.uint16)


def unstriped(offs):
    return offs[:16].T.reshape(-1).astype(np.int64)


def pack_weight(w):
    k, n = w.shape
    w = f64(np.asarray(w, np.float32).astype(ml_dtypes.bfloat16)).reshape(k // 32, 32, n)
    amax = np.abs(w).max(1)
    byte = np.clip(np.where(amax > 0, np.frexp(amax)[1] - 1 + 127 - 7, 1), 1, 254)
    scaled = (w * np.exp2(127.0 - byte)[:, None, :]).reshape(k, n).astype(np.float32)
    words = np.ascontiguousarray(scaled.reshape(k // 512, 128, 4, n).transpose(0, 1, 3, 2)).astype(ml_dtypes.float8_e4m3fn).view(np.uint8)
    return words, np.ascontiguousarray(byte.astype(np.uint8).reshape(k // 512, 16, n))


def unpack_weight(words, scales):
    g, p, n, _ = words.shape
    vals = np.ascontiguousarray(words).view(ml_dtypes.float8_e4m3fn).astype(np.float64) * np.repeat(np.exp2(scales.astype(np.float64) - 127.0), 8, axis=1)[..., None]
    return vals.transpose(0, 1, 3, 2).reshape(g * 512, n)


def sigmoid(v):
    return 1.0 / (1.0 + np.exp(-np.maximum(v, -700.0)))


K, T, S, V = 1024, 1024, 512, 512
P = 2 ** 7


def setup_inputs():
    n = np.random.standard_normal
    s = mx_kscale(K)[:, None]
    packed_xT = pack_weight(n((K, T)) * s)
    return {
        "x_words": packed_xT[0],
        "x_scales": packed_xT[1],
        "hT": (n((K, V)) / np.sqrt(K) / s).astype(np.float32),
        "diff": (np.tile(0.7 * n(T), (P, 1))).astype(np.float32),
        "guess": (np.tile(np.random.uniform(0.05, 0.3, T), (P, 1))).astype(np.float32),
        "resp": ((np.random.uniform(size=(V, S)) < 0.5) * 1.0).astype(np.float32),
        "offs": striped(np.random.permutation(T)[:S]),
    }


def reference(x_words, x_scales, hT, diff, guess, resp, offs):
    gs = f64(guess)[:1][:, unstriped(offs)]
    hTq = mxq(f64(hT), 0, "e4m3")
    xq = unpack_weight(x_words, x_scales)[:, unstriped(offs)]
    y = (hTq.T @ xq) - (f64(diff)[:1][:, unstriped(offs)])
    sg = sigmoid(1.3 * y)
    prob = gs + (-1.0 * gs + 1.0) * sg
    return ((f64(resp) - prob) * sg) / prob

@@ -1,0 +1,171 @@
+from contextlib import ExitStack
+
+import concourse.mybir as mybir
+from concourse.masks import make_identity
+
+F32 = mybir.dt.float32
+BF16 = mybir.dt.bfloat16
+I32 = mybir.dt.int32
+U32 = mybir.dt.uint32
+U16 = mybir.dt.uint16
+U8 = mybir.dt.uint8
+FP8X4 = mybir.dt.float8_e4m3fn_x4
+ACT = mybir.ActivationFunctionType
+ALU = mybir.AluOpType
+
+P = 128
+K, T, S, V = 1024, 1024, 512, 512
+PACK = 4
+PASSES = K // (P * PACK)
+ITEM_TILES = S // P
+SLOPE = 1.3
+TINY = 2.0 ** -60
+GUESS_ROW, DIFF_ROW = P - 2, P - 1
+CHUNKS = (128, 256, 128)
+CAST_ENGINE = (("scalar", "scalar"), ("scalar", "vector"), ("vector", "vector"))
+
+FLOPS = 2 * K * S * V
+BYTES = K * T + K * T // 32 + 4 * (K * V + 2 * T + 2 * V * S) + 2 * P * S // 16
+
+
+def tile_picked_yirt3_resid_p_kernel(tc, x_words, x_scales, hT, diff, guess, resp, offs, out):
+    nc = tc.nc
+    with ExitStack() as ctx:
+        keep = ctx.enter_context(tc.tile_pool(name="keep", bufs=1))
+        work = ctx.enter_context(tc.tile_pool(name="work", bufs=2))
+        psum = ctx.enter_context(tc.psum_pool(name="psum", bufs=2))
+
+        offsets = keep.tile([P, S // 16], U16, name="offsets")
+        scale_table = keep.tile([P, T], U8, name="scale_table", align_bytes=64)
+        item_table = keep.tile([P, T], F32, name="item_table")
+        word_table = [keep.tile([P, T], I32, name=f"word_table{o}") for o in range(PASSES)]
+        identity = keep.tile([P, P], F32, name="identity")
+
+        tiny = keep.tile([P, 1], F32, name="tiny")
+        warm = keep.tile([P, 2], F32, name="warm")
+        nc.gpsimd.memset(tiny[:], TINY)
+        nc.scalar.activation(warm[:, 0:1], tiny[:], ACT.Ln, bias=tiny[:])
+        nc.vector.memset(scale_table[:].bitcast(I32), 0)
+        nc.vector.memset(item_table[0:GUESS_ROW, :], 0.0)
+
+        def load_words(o):
+            nc.sync.dma_start(word_table[o][:], x_words[o].rearrange("p c r -> p (c r)").bitcast(I32))
+
+        nc.sync.dma_start(item_table[GUESS_ROW : GUESS_ROW + 1, :], guess[0:1, :])
+        nc.sync.dma_start(item_table[DIFF_ROW : DIFF_ROW + 1, :], diff[0:1, :])
+        nc.sync.dma_start(offsets[:], offs)
+        load_words(0)
+        load_words(1)
+        scale_words = x_scales.bitcast(I32)
+        for q in range(4):
+            nc.sync.dma_start(
+                scale_table[32 * q : 32 * q + 4 * PASSES, :].bitcast(I32),
+                scale_words[:, 4 * q : 4 * q + 4, :],
+            )
+        make_identity(nc, identity[:])
+
+        starts = [sum(CHUNKS[:c]) for c in range(len(CHUNKS))]
+        h_raw = {}
+        answers = {}
+
+        def load_answers(c):
+            tiles = CHUNKS[c] // P
+            both = keep.tile([P, tiles, S], F32, name=f"answers{c}")
+            rows = resp[starts[c] : starts[c] + CHUNKS[c], :]
+            nc.sync.dma_start(both[:], rows.rearrange("(a p) j -> p a j", p=P))
+            for s in range(tiles):
+                answers[starts[c] // P + s] = both[:, s, :]
+
+        for c, width in enumerate(CHUNKS):
+            for o in range(PASSES):
+                h_raw[c, o] = keep.tile([P, PACK, width], F32, name=f"h_raw{c}_{o}")
+                rows = hT[o * P * PACK : (o + 1) * P * PACK, starts[c] : starts[c] + width]
+                nc.sync.dma_start(h_raw[c, o][:], rows.rearrange("(p j) w -> p j w", j=PACK))
+            if c > 0:
+                load_answers(c - 1)
+        load_answers(len(CHUNKS) - 1)
+
+
+        item_scales = keep.tile([P, S], U8, name="item_scales", align_bytes=64)
+        item_words = [keep.tile([P, S], U32, name=f"item_words{o}", align_bytes=64) for o in range(PASSES)]
+        picked = keep.tile([P, S], F32, name="picked")
+        nc.vector.tensor_copy(picked[:], item_table[:].indirect(offsets[:]))
+        for o in range(PASSES):
+            nc.vector.tensor_copy(item_words[o][:], word_table[o][:].bitcast(U32).indirect(offsets[:]))
+        nc.vector.tensor_copy(item_scales[:], scale_table[:].indirect(offsets[:]))
+
+        turned = psum.tile([P, ITEM_TILES, P], F32, name="turned", tag="ratio")
+        for i in range(ITEM_TILES):
+            nc.tensor.transpose(turned[:, i, :], picked[:, i * P : (i + 1) * P], identity[:])
+        bias_sg = keep.tile([P, ITEM_TILES], F32, name="bias_sg")
+        bias_ratio = keep.tile([P, ITEM_TILES], F32, name="bias_ratio")
+        log_guess = keep.tile([P, ITEM_TILES], F32, name="log_guess")
+        nc.scalar.activation(log_guess[:], turned[:, :, GUESS_ROW], ACT.Ln, bias=tiny[:])
+        nc.scalar.activation(bias_sg[:], turned[:, :, DIFF_ROW], ACT.Copy, scale=-SLOPE)
+        nc.scalar.activation(warm[:, 1:2], log_guess[:, 0:1], ACT.Sigmoid)
+        nc.gpsimd.tensor_tensor(bias_ratio[:], bias_sg[:], log_guess[:], ALU.subtract)
+
+        def quantise(c):
+            width = CHUNKS[c]
+            codes = keep.tile([P, PASSES, width], U32, name=f"h_codes{c}", align_bytes=64)
+            scales = keep.tile([P, PASSES, width], U8, name=f"h_scales{c}", align_bytes=64)
+            for o in range(PASSES):
+                grouped = keep.tile([P, width, PACK], BF16, name=f"h_grouped{c}_{o}", align_bytes=64)
+                dst = grouped[:].rearrange("p (w i) j -> p w j i", i=4)
+                src = h_raw[c, o][:].rearrange("p j (w i) -> p w j i", i=4)
+                if CAST_ENGINE[c][o] == "scalar":
+                    nc.scalar.copy(dst, src)
+                else:
+                    nc.vector.tensor_copy(dst, src)
+                nc.vector.quantize_mx(
+                    out=codes[:, o, :].bitcast(FP8X4),
+                    scales=scales[:, o, :],
+                    in_=grouped[:].rearrange("p w j -> p (w j)"),
+                )
+            return codes, scales
+
+        def multiply(c, codes, scales):
+            width = CHUNKS[c]
+            per_bank = S // width
+            banks = [psum.tile([P, per_bank, width], F32, name=f"logit{c}_{b}", tag=f"logit{b}") for b in range(ITEM_TILES // per_bank)]
+            logit = [banks[i // per_bank][:, i % per_bank, :] for i in range(ITEM_TILES)]
+            for i in range(ITEM_TILES):
+                items = slice(i * P, (i + 1) * P)
+                for o in range(PASSES):
+                    nc.tensor.matmul_mx(
+                        out=logit[i],
+                        lhsT=item_words[o][:, items].bitcast(FP8X4),
+                        lhsT_scale=item_scales[4 * o : P, items],
+                        rhs=codes[:, o, :].bitcast(FP8X4),
+                        rhs_scale=scales[:, o, :],
+                        start=(o == 0),
+                        stop=(o == PASSES - 1),
+                    )
+            return logit
+
+        def finish(c, logit):
+            width = CHUNKS[c]
+            ratio_t = work.tile([P, ITEM_TILES, width], F32, name="ratio_t")
+            sg_t = work.tile([P, ITEM_TILES, width], F32, name="sg_t")
+            for dst, bias in ((ratio_t, bias_ratio), (sg_t, bias_sg)):
+                for i in range(ITEM_TILES):
+                    nc.scalar.activation(dst[:, i, :], logit[i], ACT.Sigmoid, bias=bias[:, i : i + 1], scale=SLOPE)
+            for s in range(width // P):
+                a = starts[c] // P + s
+                students = slice(s * P, (s + 1) * P)
+                ratio = psum.tile([P, S], F32, name="ratio", tag="ratio")
+                sg = psum.tile([P, S], F32, name="sg", tag="sg")
+                for dst, src in ((ratio, ratio_t), (sg, sg_t)):
+                    for i in range(ITEM_TILES):
+                        nc.tensor.transpose(dst[:, i * P : (i + 1) * P], src[:, i, students], identity[:])
+                weighted = work.tile([P, S], F32, name="weighted")
+                result = keep.tile([P, S], F32, name=f"result{a}")
+                nc.vector.tensor_tensor(weighted[:], ratio[:], answers[a], ALU.mult)
+                nc.vector.tensor_tensor(result[:], weighted[:], sg[:], ALU.subtract)
+                nc.sync.dma_start(out[a * P : (a + 1) * P, :], result[:])
+
+        ready = multiply(0, *quantise(0))
+        for c in range(len(CHUNKS)):
+            coming = multiply(c + 1, *quantise(c + 1)) if c + 1 < len(CHUNKS) else None
+            finish(c, ready)
+            ready = coming

@@ -21,8 +21,7 @@ ITEM_TILES = S // P
 SLOPE = 1.3
 TINY = 2.0 ** -60
 GUESS_ROW, DIFF_ROW = P - 2, P - 1
-CHUNKS = (128, 256, 128)
-CAST_ENGINE = (("scalar", "scalar"), ("scalar", "vector"), ("vector", "vector"))
+HALF = V // 2
 
 FLOPS = 2 * K * S * V
 BYTES = K * T + K * T // 32 + 4 * (K * V + 2 * T + 2 * V * S) + 2 * P * S // 16
@@ -32,7 +31,6 @@ def tile_picked_yirt3_resid_p_kernel(tc, x_words, x_scales, hT, diff, guess, res
     nc = tc.nc
     with ExitStack() as ctx:
         keep = ctx.enter_context(tc.tile_pool(name="keep", bufs=1))
-        work = ctx.enter_context(tc.tile_pool(name="work", bufs=2))
         psum = ctx.enter_context(tc.psum_pool(name="psum", bufs=2))
 
         offsets = keep.tile([P, S // 16], U16, name="offsets")
@@ -40,61 +38,60 @@ def tile_picked_yirt3_resid_p_kernel(tc, x_words, x_scales, hT, diff, guess, res
         item_table = keep.tile([P, T], F32, name="item_table")
         word_table = [keep.tile([P, T], I32, name=f"word_table{o}") for o in range(PASSES)]
         identity = keep.tile([P, P], F32, name="identity")
-
         tiny = keep.tile([P, 1], F32, name="tiny")
         warm = keep.tile([P, 2], F32, name="warm")
+
         nc.gpsimd.memset(tiny[:], TINY)
         nc.scalar.activation(warm[:, 0:1], tiny[:], ACT.Ln, bias=tiny[:])
         nc.vector.memset(scale_table[:].bitcast(I32), 0)
         nc.vector.memset(item_table[0:GUESS_ROW, :], 0.0)
+        make_identity(nc, identity[:])
 
         def load_words(o):
             nc.sync.dma_start(word_table[o][:], x_words[o].rearrange("p c r -> p (c r)").bitcast(I32))
 
+        def load_h(o, first, width):
+            raw = keep.tile([P, PACK, width], F32, name=f"h_raw{o}_{first}")
+            rows = hT[o * P * PACK : (o + 1) * P * PACK, first : first + width]
+            nc.sync.dma_start(raw[:], rows.rearrange("(p j) w -> p j w", j=PACK))
+            return raw
+
+        def load_scales(q):
+            nc.sync.dma_start(
+                scale_table[32 * q : 32 * q + 4 * PASSES, :].bitcast(I32),
+                x_scales.bitcast(I32)[:, 4 * q : 4 * q + 4, :],
+            )
+
+        def load_answers(c):
+            both = keep.tile([P, HALF // P, S], F32, name=f"answers{c}")
+            nc.sync.dma_start(both[:], resp[c * HALF : (c + 1) * HALF, :].rearrange("(a p) j -> p a j", p=P))
+            return both
+
         nc.sync.dma_start(item_table[GUESS_ROW : GUESS_ROW + 1, :], guess[0:1, :])
         nc.sync.dma_start(item_table[DIFF_ROW : DIFF_ROW + 1, :], diff[0:1, :])
         nc.sync.dma_start(offsets[:], offs)
+        early = [load_h(0, 0, HALF)]
         load_words(0)
-        load_words(1)
-        scale_words = x_scales.bitcast(I32)
         for q in range(4):
-            nc.sync.dma_start(
-                scale_table[32 * q : 32 * q + 4 * PASSES, :].bitcast(I32),
-                scale_words[:, 4 * q : 4 * q + 4, :],
-            )
-        make_identity(nc, identity[:])
-
-        starts = [sum(CHUNKS[:c]) for c in range(len(CHUNKS))]
-        h_raw = {}
-        answers = {}
-
-        def load_answers(c):
-            tiles = CHUNKS[c] // P
-            both = keep.tile([P, tiles, S], F32, name=f"answers{c}")
-            rows = resp[starts[c] : starts[c] + CHUNKS[c], :]
-            nc.sync.dma_start(both[:], rows.rearrange("(a p) j -> p a j", p=P))
-            for s in range(tiles):
-                answers[starts[c] // P + s] = both[:, s, :]
-
-        for c, width in enumerate(CHUNKS):
-            for o in range(PASSES):
-                h_raw[c, o] = keep.tile([P, PACK, width], F32, name=f"h_raw{c}_{o}")
-                rows = hT[o * P * PACK : (o + 1) * P * PACK, starts[c] : starts[c] + width]
-                nc.sync.dma_start(h_raw[c, o][:], rows.rearrange("(p j) w -> p j w", j=PACK))
-            if c > 0:
-                load_answers(c - 1)
-        load_answers(len(CHUNKS) - 1)
-
+            load_scales(q)
+        early.append(load_h(1, 0, HALF))
+        load_words(1)
+        late = [load_h(o, HALF, HALF) for o in range(PASSES)]
+        answers = [load_answers(c) for c in range(2)]
 
         item_scales = keep.tile([P, S], U8, name="item_scales", align_bytes=64)
         item_words = [keep.tile([P, S], U32, name=f"item_words{o}", align_bytes=64) for o in range(PASSES)]
         picked = keep.tile([P, S], F32, name="picked")
         nc.vector.tensor_copy(picked[:], item_table[:].indirect(offsets[:]))
-        for o in range(PASSES):
-            nc.vector.tensor_copy(item_words[o][:], word_table[o][:].bitcast(U32).indirect(offsets[:]))
+
+        def gather(dst, table, part):
+            entries = slice(part * S // 2, (part + 1) * S // 2)
+            nc.vector.tensor_copy(dst[:, entries], table.indirect(offsets[:, part * S // 32 : (part + 1) * S // 32]))
+
+        nc.vector.tensor_copy(item_words[0][:], word_table[0][:].bitcast(U32).indirect(offsets[:]))
         nc.vector.tensor_copy(item_scales[:], scale_table[:].indirect(offsets[:]))
 
-        turned = psum.tile([P, ITEM_TILES, P], F32, name="turned", tag="ratio")
+        turned = psum.tile([P, ITEM_TILES, P], F32, name="turned", tag="spare")
         for i in range(ITEM_TILES):
             nc.tensor.transpose(turned[:, i, :], picked[:, i * P : (i + 1) * P], identity[:])
         bias_sg = keep.tile([P, ITEM_TILES], F32, name="bias_sg")
@@ -102,70 +99,81 @@ def tile_picked_yirt3_resid_p_kernel(tc, x_words, x_scales, hT, diff, guess, res
         log_guess = keep.tile([P, ITEM_TILES], F32, name="log_guess")
         nc.scalar.activation(log_guess[:], turned[:, :, GUESS_ROW], ACT.Ln, bias=tiny[:])
         nc.scalar.activation(bias_sg[:], turned[:, :, DIFF_ROW], ACT.Copy, scale=-SLOPE)
-        nc.scalar.activation(warm[:, 1:2], log_guess[:, 0:1], ACT.Sigmoid)
         nc.gpsimd.tensor_tensor(bias_ratio[:], bias_sg[:], log_guess[:], ALU.subtract)
 
-        def quantise(c):
-            width = CHUNKS[c]
-            codes = keep.tile([P, PASSES, width], U32, name=f"h_codes{c}", align_bytes=64)
-            scales = keep.tile([P, PASSES, width], U8, name=f"h_scales{c}", align_bytes=64)
-            for o in range(PASSES):
-                grouped = keep.tile([P, width, PACK], BF16, name=f"h_grouped{c}_{o}", align_bytes=64)
-                dst = grouped[:].rearrange("p (w i) j -> p w j i", i=4)
-                src = h_raw[c, o][:].rearrange("p j (w i) -> p w j i", i=4)
-                if CAST_ENGINE[c][o] == "scalar":
-                    nc.scalar.copy(dst, src)
-                else:
-                    nc.vector.tensor_copy(dst, src)
-                nc.vector.quantize_mx(
-                    out=codes[:, o, :].bitcast(FP8X4),
-                    scales=scales[:, o, :],
-                    in_=grouped[:].rearrange("p w j -> p (w j)"),
-                )
-            return codes, scales
+        codes = [keep.tile([P, PASSES, HALF], U32, name=f"h_codes{c}", align_bytes=64) for c in range(2)]
+        scales = [keep.tile([P, PASSES, HALF], U8, name=f"h_scales{c}", align_bytes=64) for c in range(2)]
+        grouped = {(0, o): keep.tile([P, HALF, PACK], BF16, name=f"h_grouped0_{o}", align_bytes=64) for o in range(PASSES)}
+        grouped_late = keep.tile([P, PASSES, HALF, PACK], BF16, name="h_grouped1", align_bytes=64)
 
-        def multiply(c, codes, scales):
-            width = CHUNKS[c]
-            per_bank = S // width
-            banks = [psum.tile([P, per_bank, width], F32, name=f"logit{c}_{b}", tag=f"logit{b}") for b in range(ITEM_TILES // per_bank)]
-            logit = [banks[i // per_bank][:, i % per_bank, :] for i in range(ITEM_TILES)]
-            for i in range(ITEM_TILES):
+        def interleave(copy, dst, raw):
+            copy(dst.rearrange("p (w i) j -> p w j i", i=4), raw.rearrange("p j (w i) -> p w j i", i=4))
+
+        def quantise(c, o):
+            nc.vector.quantize_mx(
+                out=codes[c][:, o, :].bitcast(FP8X4),
+                scales=scales[c][:, o, :],
+                in_=grouped[c, o][:].rearrange("p w j -> p (w j)"),
+            )
+
+        for o in range(PASSES):
+            interleave(nc.scalar.copy, grouped[0, o][:], early[o][:])
+            quantise(0, o)
+        nc.scalar.activation(warm[:, 1:2], grouped[0, 1][:, HALF - 1, 0:1], ACT.Sigmoid, bias=log_guess[:, 0:1])
+        gather(item_words[1], word_table[1][:].bitcast(U32), 0)
+        gather(item_words[1], word_table[1][:].bitcast(U32), 1)
+
+        def multiply(c, part):
+            logit = psum.tile([P, 2, HALF], F32, name=f"logit{part}", tag=f"logit{part}")
+            for n in range(2):
+                i = 2 * part + n
                 items = slice(i * P, (i + 1) * P)
                 for o in range(PASSES):
                     nc.tensor.matmul_mx(
-                        out=logit[i],
+                        out=logit[:, n, :],
                         lhsT=item_words[o][:, items].bitcast(FP8X4),
                         lhsT_scale=item_scales[4 * o : P, items],
-                        rhs=codes[:, o, :].bitcast(FP8X4),
-                        rhs_scale=scales[:, o, :],
+                        rhs=codes[c][:, o, :].bitcast(FP8X4),
+                        rhs_scale=scales[c][:, o, :],
                         start=(o == 0),
                         stop=(o == PASSES - 1),
                     )
             return logit
 
-        def finish(c, logit):
-            width = CHUNKS[c]
-            ratio_t = work.tile([P, ITEM_TILES, width], F32, name="ratio_t")
-            sg_t = work.tile([P, ITEM_TILES, width], F32, name="sg_t")
-            for dst, bias in ((ratio_t, bias_ratio), (sg_t, bias_sg)):
-                for i in range(ITEM_TILES):
-                    nc.scalar.activation(dst[:, i, :], logit[i], ACT.Sigmoid, bias=bias[:, i : i + 1], scale=SLOPE)
-            for s in range(width // P):
-                a = starts[c] // P + s
-                students = slice(s * P, (s + 1) * P)
-                ratio = psum.tile([P, S], F32, name="ratio", tag="ratio")
-                sg = psum.tile([P, S], F32, name="sg", tag="sg")
-                for dst, src in ((ratio, ratio_t), (sg, sg_t)):
-                    for i in range(ITEM_TILES):
-                        nc.tensor.transpose(dst[:, i * P : (i + 1) * P], src[:, i, students], identity[:])
-                weighted = work.tile([P, S], F32, name="weighted")
-                result = keep.tile([P, S], F32, name=f"result{a}")
-                nc.vector.tensor_tensor(weighted[:], ratio[:], answers[a], ALU.mult)
-                nc.vector.tensor_tensor(result[:], weighted[:], sg[:], ALU.subtract)
-                nc.sync.dma_start(out[a * P : (a + 1) * P, :], result[:])
+        def sigmoid_turned(tag, c, part, logit, bias):
+            values = keep.tile([P, 2, HALF], F32, name=f"{tag}_t{c}_{part}")
+            bank = psum.tile([P, 2, S // 2], F32, name=tag, tag="spare" if (tag, c) == ("ratio", 1) else "shared")
+            for n in range(2):
+                i = 2 * part + n
+                nc.scalar.activation(values[:, n, :], logit[:, n, :], ACT.Sigmoid, bias=bias[:, i : i + 1], scale=SLOPE)
+            for n in range(2):
+                for s in range(2):
+                    nc.tensor.transpose(bank[:, s, n * P : (n + 1) * P], values[:, n, s * P : (s + 1) * P], identity[:])
+            return bank
 
-        ready = multiply(0, *quantise(0))
-        for c in range(len(CHUNKS)):
-            coming = multiply(c + 1, *quantise(c + 1)) if c + 1 < len(CHUNKS) else None
-            finish(c, ready)
-            ready = coming
+        def finish(c, logit):
+            weighted = []
+            for part in range(2):
+                cols = slice(part * S // 2, (part + 1) * S // 2)
+                ratio = sigmoid_turned("ratio", c, part, logit[part], bias_ratio)
+                weighted.append(keep.tile([P, 2, S // 2], F32, name=f"weighted{c}_{part}"))
+                nc.vector.tensor_tensor(weighted[part][:], ratio[:], answers[c][:, :, cols], ALU.mult)
+            for part in range(2):
+                cols = slice(part * S // 2, (part + 1) * S // 2)
+                sg = sigmoid_turned("sg", c, part, logit[part], bias_sg)
+                result = keep.tile([P, 2, S // 2], F32, name=f"result{c}_{part}")
+                nc.vector.tensor_tensor(result[:], weighted[part][:], sg[:], ALU.subtract)
+                rows = out[c * HALF : (c + 1) * HALF, cols]
+                nc.sync.dma_start(rows.rearrange("(s p) j -> p s j", p=P), result[:])
+
+        logit0 = [multiply(0, part) for part in range(2)]
+        for o in range(PASSES):
+            interleave(nc.vector.tensor_copy, grouped_late[:, o], late[o][:])
+        nc.vector.quantize_mx(
+            out=codes[1][:].rearrange("p o w -> p (o w)").bitcast(FP8X4),
+            scales=scales[1][:].rearrange("p o w -> p (o w)"),
+            in_=grouped_late[:].rearrange("p o w j -> p (o w j)"),
+        )
+        logit1 = [multiply(1, part) for part in range(2)]
+        finish(0, logit0)
+        finish(1, logit1)

from contextlib import ExitStack

import concourse.mybir as mybir
from concourse.masks import make_identity

F32 = mybir.dt.float32
BF16 = mybir.dt.bfloat16
I32 = mybir.dt.int32
U32 = mybir.dt.uint32
U16 = mybir.dt.uint16
U8 = mybir.dt.uint8
FP8X4 = mybir.dt.float8_e4m3fn_x4
ACT = mybir.ActivationFunctionType
ALU = mybir.AluOpType

P = 128
K, T, S, V = 1024, 1024, 512, 512
PACK = 4
PASSES = K // (P * PACK)
ITEM_TILES = S // P
SLOPE = 1.3
TINY = 2.0 ** -60
GUESS_ROW, DIFF_ROW = P - 2, P - 1
HALF = V // 2

FLOPS = 2 * K * S * V
BYTES = K * T + K * T // 32 + 4 * (K * V + 2 * T + 2 * V * S) + 2 * P * S // 16


def tile_picked_yirt3_resid_p_kernel(tc, x_words, x_scales, hT, diff, guess, resp, offs, out):
    nc = tc.nc
    with ExitStack() as ctx:
        keep = ctx.enter_context(tc.tile_pool(name="keep", bufs=1))
        psum = ctx.enter_context(tc.psum_pool(name="psum", bufs=2))

        offsets = keep.tile([P, S // 16], U16, name="offsets")
        scale_table = keep.tile([P, T], U8, name="scale_table", align_bytes=64)
        item_table = keep.tile([P, T], F32, name="item_table")
        word_table = [keep.tile([P, T], I32, name=f"word_table{o}") for o in range(PASSES)]
        identity = keep.tile([P, P], F32, name="identity")
        tiny = keep.tile([P, 1], F32, name="tiny")
        warm = keep.tile([P, 2], F32, name="warm")

        nc.gpsimd.memset(tiny[:], TINY)
        nc.scalar.activation(warm[:, 0:1], tiny[:], ACT.Ln, bias=tiny[:])
        nc.vector.memset(scale_table[:].bitcast(I32), 0)
        nc.vector.memset(item_table[0:GUESS_ROW, :], 0.0)
        make_identity(nc, identity[:])

        def load_words(o):
            nc.sync.dma_start(word_table[o][:], x_words[o].rearrange("p c r -> p (c r)").bitcast(I32))

        def load_h(o, first, width):
            raw = keep.tile([P, PACK, width], F32, name=f"h_raw{o}_{first}")
            rows = hT[o * P * PACK : (o + 1) * P * PACK, first : first + width]
            nc.sync.dma_start(raw[:], rows.rearrange("(p j) w -> p j w", j=PACK))
            return raw

        def load_scales(q):
            nc.sync.dma_start(
                scale_table[32 * q : 32 * q + 4 * PASSES, :].bitcast(I32),
                x_scales.bitcast(I32)[:, 4 * q : 4 * q + 4, :],
            )

        def load_answers(c):
            both = keep.tile([P, HALF // P, S], F32, name=f"answers{c}")
            nc.sync.dma_start(both[:], resp[c * HALF : (c + 1) * HALF, :].rearrange("(a p) j -> p a j", p=P))
            return both

        nc.sync.dma_start(item_table[GUESS_ROW : GUESS_ROW + 1, :], guess[0:1, :])
        nc.sync.dma_start(item_table[DIFF_ROW : DIFF_ROW + 1, :], diff[0:1, :])
        nc.sync.dma_start(offsets[:], offs)
        early = [load_h(0, 0, HALF)]
        load_words(0)
        for q in range(4):
            load_scales(q)
        early.append(load_h(1, 0, HALF))
        load_words(1)
        late = [load_h(o, HALF, HALF) for o in range(PASSES)]
        answers = [load_answers(c) for c in range(2)]

        item_scales = keep.tile([P, S], U8, name="item_scales", align_bytes=64)
        item_words = [keep.tile([P, S], U32, name=f"item_words{o}", align_bytes=64) for o in range(PASSES)]
        picked = keep.tile([P, S], F32, name="picked")
        nc.vector.tensor_copy(picked[:], item_table[:].indirect(offsets[:]))

        def gather(dst, table, part):
            entries = slice(part * S // 2, (part + 1) * S // 2)
            nc.vector.tensor_copy(dst[:, entries], table.indirect(offsets[:, part * S // 32 : (part + 1) * S // 32]))

        nc.vector.tensor_copy(item_words[0][:], word_table[0][:].bitcast(U32).indirect(offsets[:]))
        nc.vector.tensor_copy(item_scales[:], scale_table[:].indirect(offsets[:]))

        turned = psum.tile([P, ITEM_TILES, P], F32, name="turned", tag="spare")
        for i in range(ITEM_TILES):
            nc.tensor.transpose(turned[:, i, :], picked[:, i * P : (i + 1) * P], identity[:])
        bias_sg = keep.tile([P, ITEM_TILES], F32, name="bias_sg")
        bias_ratio = keep.tile([P, ITEM_TILES], F32, name="bias_ratio")
        log_guess = keep.tile([P, ITEM_TILES], F32, name="log_guess")
        nc.scalar.activation(log_guess[:], turned[:, :, GUESS_ROW], ACT.Ln, bias=tiny[:])
        nc.scalar.activation(bias_sg[:], turned[:, :, DIFF_ROW], ACT.Copy, scale=-SLOPE)
        nc.gpsimd.tensor_tensor(bias_ratio[:], bias_sg[:], log_guess[:], ALU.subtract)

        codes = [keep.tile([P, PASSES, HALF], U32, name=f"h_codes{c}", align_bytes=64) for c in range(2)]
        scales = [keep.tile([P, PASSES, HALF], U8, name=f"h_scales{c}", align_bytes=64) for c in range(2)]
        grouped = {(0, o): keep.tile([P, HALF, PACK], BF16, name=f"h_grouped0_{o}", align_bytes=64) for o in range(PASSES)}
        grouped_late = keep.tile([P, PASSES, HALF, PACK], BF16, name="h_grouped1", align_bytes=64)

        def interleave(copy, dst, raw):
            copy(dst.rearrange("p (w i) j -> p w j i", i=4), raw.rearrange("p j (w i) -> p w j i", i=4))

        def quantise(c, o):
            nc.vector.quantize_mx(
                out=codes[c][:, o, :].bitcast(FP8X4),
                scales=scales[c][:, o, :],
                in_=grouped[c, o][:].rearrange("p w j -> p (w j)"),
            )

        for o in range(PASSES):
            interleave(nc.scalar.copy, grouped[0, o][:], early[o][:])
            quantise(0, o)
        nc.scalar.activation(warm[:, 1:2], grouped[0, 1][:, HALF - 1, 0:1], ACT.Sigmoid, bias=log_guess[:, 0:1])
        gather(item_words[1], word_table[1][:].bitcast(U32), 0)
        gather(item_words[1], word_table[1][:].bitcast(U32), 1)

        def multiply(c, part):
            logit = psum.tile([P, 2, HALF], F32, name=f"logit{part}", tag=f"logit{part}")
            for n in range(2):
                i = 2 * part + n
                items = slice(i * P, (i + 1) * P)
                for o in range(PASSES):
                    nc.tensor.matmul_mx(
                        out=logit[:, n, :],
                        lhsT=item_words[o][:, items].bitcast(FP8X4),
                        lhsT_scale=item_scales[4 * o : P, items],
                        rhs=codes[c][:, o, :].bitcast(FP8X4),
                        rhs_scale=scales[c][:, o, :],
                        start=(o == 0),
                        stop=(o == PASSES - 1),
                    )
            return logit

        def sigmoid_turned(tag, c, part, logit, bias):
            values = keep.tile([P, 2, HALF], F32, name=f"{tag}_t{c}_{part}")
            bank = psum.tile([P, 2, S // 2], F32, name=tag, tag="spare" if (tag, c) == ("ratio", 1) else "shared")
            for n in range(2):
                i = 2 * part + n
                nc.scalar.activation(values[:, n, :], logit[:, n, :], ACT.Sigmoid, bias=bias[:, i : i + 1], scale=SLOPE)
            for n in range(2):
                for s in range(2):
                    nc.tensor.transpose(bank[:, s, n * P : (n + 1) * P], values[:, n, s * P : (s + 1) * P], identity[:])
            return bank

        def finish(c, logit):
            weighted = []
            for part in range(2):
                cols = slice(part * S // 2, (part + 1) * S // 2)
                ratio = sigmoid_turned("ratio", c, part, logit[part], bias_ratio)
                weighted.append(keep.tile([P, 2, S // 2], F32, name=f"weighted{c}_{part}"))
                nc.vector.tensor_tensor(weighted[part][:], ratio[:], answers[c][:, :, cols], ALU.mult)
            for part in range(2):
                cols = slice(part * S // 2, (part + 1) * S // 2)
                sg = sigmoid_turned("sg", c, part, logit[part], bias_sg)
                result = keep.tile([P, 2, S // 2], F32, name=f"result{c}_{part}")
                nc.vector.tensor_tensor(result[:], weighted[part][:], sg[:], ALU.subtract)
                rows = out[c * HALF : (c + 1) * HALF, cols]
                nc.sync.dma_start(rows.rearrange("(s p) j -> p s j", p=P), result[:])

        logit0 = [multiply(0, part) for part in range(2)]
        for o in range(PASSES):
            interleave(nc.vector.tensor_copy, grouped_late[:, o], late[o][:])
        nc.vector.quantize_mx(
            out=codes[1][:].rearrange("p o w -> p (o w)").bitcast(FP8X4),
            scales=scales[1][:].rearrange("p o w -> p (o w)"),
            in_=grouped_late[:].rearrange("p o w j -> p (o w j)"),
        )
        logit1 = [multiply(1, part) for part in range(2)]
        finish(0, logit0)
        finish(1, logit1)
